import numpy as np
import ml_dtypes


def mxq(x, axis, fmt="e4m3"):
    dtype, down = {"e4m3": (ml_dtypes.float8_e4m3fn, 7), "e5m2": (ml_dtypes.float8_e5m2, 14)}[fmt]
    v = np.moveaxis(np.asarray(x, np.float32).astype(ml_dtypes.bfloat16).astype(np.float64), axis, -1)
    blocks = v.reshape(v.shape[:-1] + (-1, 32))
    amax = np.abs(blocks).max(-1, keepdims=True)
    byte = np.maximum(np.where(amax > 0, np.frexp(amax)[1] - 1 + 127, 0) - down, 1)
    scale = np.exp2(byte - 127.0)
    codes = (blocks / scale).astype(np.float32).astype(dtype).astype(np.float64)
    return np.moveaxis((codes * scale).reshape(v.shape), -1, axis)


WIDE = False


def mx_kscale(k):
    if not WIDE:
        return np.ones(k)
    levels = np.array([10, -10, 5, -5, 0])
    if k % 512:
        return np.exp2(np.random.permutation(np.resize(levels, k // 32))).repeat(32)
    a = np.empty((k // 512, 16))
    for p in range(k // 512):
        a[p, :8] = np.random.permutation(np.resize(levels, 8))
        for g in range(8):
            far = levels[np.abs(levels - a[p, g]) >= 10]
            a[p, g + 8] = far[np.random.randint(len(far))]
    return np.exp2(a.ravel()).repeat(32)


def f64(x):
    return np.asarray(x).astype(np.float64)


def striped(idx):
    return np.tile(np.asarray(idx).reshape(-1, 16).T, (8, 1)).astype(np.uint16)


def unstriped(offs):
    return offs[:16].T.reshape(-1).astype(np.int64)


E2M1 = np.array([0.0, 0.5, 1.0, 1.5, 2.0, 3.0, 4.0, 6.0, -0.0, -0.5, -1.0, -1.5, -2.0, -3.0, -4.0, -6.0])


def pack_weight(w, fmt):
    k, n = w.shape
    w = f64(np.asarray(w, np.float32).astype(ml_dtypes.bfloat16)).reshape(k // 32, 32, n)
    amax = np.abs(w).max(1)
    if fmt == "e4m3":
        byte = np.frexp(amax)[1] - 1 + 127 - 7
    else:
        mant, ex = np.frexp(amax / 6.0)
        byte = np.where(mant > 0.5, ex, ex - 1) + 127
    byte = np.clip(np.where(amax > 0, byte, 1), 1, 254)
    scaled = (w * np.exp2(127.0 - byte)[:, None, :]).reshape(k, n).astype(np.float32)
    by_word = np.ascontiguousarray(scaled.reshape(k // 512, 128, 4, n).transpose(0, 1, 3, 2))
    if fmt == "e4m3":
        words = by_word.astype(ml_dtypes.float8_e4m3fn).view(np.uint8)
    else:
        c = by_word.astype(ml_dtypes.float4_e2m1fn).view(np.uint8) & 0xF
        words = (c[..., 0::2] | (c[..., 1::2] << 4)).reshape(k // 512, 128, 2 * n)
    return np.ascontiguousarray(words), np.ascontiguousarray(byte.astype(np.uint8).reshape(k // 512, 16, n))


def unpack_weight(words, scales, fmt):
    g, _, n = scales.shape
    words = np.ascontiguousarray(words).reshape(g, 128, n, -1)
    if fmt == "e4m3":
        vals = words.view(ml_dtypes.float8_e4m3fn).astype(np.float64)
    else:
        nib = np.empty((g, 128, n, 4), np.uint8)
        nib[..., 0::2] = words & 0xF
        nib[..., 1::2] = words >> 4
        vals = E2M1[nib]
    vals = vals * np.repeat(np.exp2(scales.astype(np.float64) - 127.0), 8, axis=1)[..., None]
    return vals.transpose(0, 1, 3, 2).reshape(g * 512, n)


def silu(v):
    return v / (1.0 + np.exp(-v))


B, N, T, D, NQ = 1, 512, 2048, 512, 512
DV = 512


def sgn(shape):
    return np.random.uniform(0.5, 2.0, shape) * np.where(np.random.standard_normal(shape) < 0, -1.0, 1.0)


def setup_inputs():
    n = np.random.standard_normal
    idx = np.random.permutation(T)[:B * N]
    s = mx_kscale(D)[:, None]
    u = mx_kscale(N)
    ut = np.ones(T)
    ut[idx] = u
    kp = pack_weight(n((D, T)) / s, "e4m3")
    cp = pack_weight(n((D, T)) / s, "e4m3")
    return {
        "qT": (n((B, D, NQ)) * s * (1.00 / np.sqrt(D))).astype(np.float32),
        "k_words": kp[0],
        "k_scales": kp[1],
        "c_words": cp[0],
        "c_scales": cp[1],
        "vT": (n((DV, T)) / ut).astype(np.float32),
        "us": (sgn((B, N, 1)) * u[:, None]).astype(np.float32),
        "offs": striped(idx),
    }


def reference(qT, k_words, k_scales, c_words, c_scales, vT, us, offs):
    idx = unstriped(offs)
    pick = lambda x, which: x[:, which].reshape(x.shape[0], B, -1).transpose(1, 0, 2)
    k = unpack_weight(k_words, k_scales, "e4m3")
    kg = pick(k, idx)
    c = unpack_weight(c_words, c_scales, "e4m3")
    cg = pick(c, idx)
    qq = mxq(f64(qT), 1, "e4m3")
    a = kg.transpose(0, 2, 1) @ qq
    z = cg.transpose(0, 2, 1) @ qq
    y = silu(a) * z * f64(us)
    wq = mxq(y, 1, "e4m3")
    o = wq.transpose(0, 2, 1) @ mxq(pick(f64(vT), idx).transpose(0, 2, 1), 1, "e4m3")
    return o

@@ -1,0 +1,191 @@
+from contextlib import ExitStack
+
+import concourse.mybir as mybir
+from concourse.masks import make_identity
+
+F32 = mybir.dt.float32
+BF16 = mybir.dt.bfloat16
+I32 = mybir.dt.int32
+U32 = mybir.dt.uint32
+U16 = mybir.dt.uint16
+U8 = mybir.dt.uint8
+FP8X4 = mybir.dt.float8_e4m3fn_x4
+MULT = mybir.AluOpType.mult
+SILU = mybir.ActivationFunctionType.Silu
+
+P = 128
+PACK = 4
+SLOTS = 512
+NEURONS = 2048
+QUERIES = 512
+OUTPUTS = 512
+QUADRANTS = 4
+FLOPS = 3 * 2 * 512 * 512 * 512
+
+
+def tile_attend_mlp_swiglu_topk_kernel(tc, qT, k_words, k_scales, c_words, c_scales, vT, us, offs, out):
+    nc = tc.nc
+    blocks = OUTPUTS // P
+    q_tiles = QUERIES // P
+    with ExitStack() as ctx:
+        sb = ctx.enter_context(tc.tile_pool(name="sb", bufs=1))
+        ps = ctx.enter_context(tc.psum_pool(name="ps", bufs=1))
+
+        offsets = sb.tile([P, SLOTS // 16], U16, name="offsets")
+        nc.sync.dma_start(offsets[:], offs)
+        q_raw = sb.tile([P, PACK, QUERIES], F32, name="q_raw")
+        nc.sync.dma_start(q_raw[:], qT[0].rearrange("(p j) q -> p j q", j=PACK))
+
+        def load_scales(name, scales, row0):
+            table = sb.tile([P, NEURONS], U8, name=name)
+            nc.vector.memset(table[:].bitcast(I32), 0)
+            rows = scales[0].bitcast(I32)
+            for quad in range(QUADRANTS):
+                first = 32 * quad + row0
+                queue = nc.gpsimd if quad == QUADRANTS - 1 else nc.scalar
+                queue.dma_start(table[first : first + 4, :].bitcast(I32), rows[4 * quad : 4 * quad + 4, :])
+            return table
+
+        def load_words(name, words):
+            table = sb.tile([P, NEURONS], I32, name=name)
+            nc.sync.dma_start(table[:], words[0].rearrange("p n t -> p (n t)").bitcast(I32))
+            return table
+
+        k_scale_table = load_scales("k_scale_table", k_scales, 0)
+        k_word_table = load_words("k_word_table", k_words)
+        c_scale_table = load_scales("c_scale_table", c_scales, 4)
+        c_word_table = load_words("c_word_table", c_words)
+        slot_scale = sb.tile([P, PACK], F32, name="slot_scale")
+        nc.gpsimd.dma_start(slot_scale[:], us[0].rearrange("(p r) o -> p (r o)", r=PACK))
+        v_tables = []
+        for j in range(blocks):
+            v_table = sb.tile([P, NEURONS], F32, name="v_table%d" % j, tag="v_table%d" % j, align_bytes=64)
+            nc.sync.dma_start(v_table[:], vT[j * P : (j + 1) * P, :])
+            v_tables.append(v_table)
+
+        ident = sb.tile([P, P], F32, name="ident")
+        make_identity(nc, ident[:])
+
+        def gather_scales(name, table):
+            picked = sb.tile([P, SLOTS], U8, name=name + "_picked")
+            nc.vector.tensor_copy(picked[:], table[:].indirect(offsets[:]))
+            dealt = sb.tile([P, SLOTS], U8, name=name + "_dealt", align_bytes=64)
+            nc.vector.tensor_copy(
+                dealt[:].rearrange("p (r s) -> p s r", r=PACK), picked[:].rearrange("p (s r) -> p s r", r=PACK)
+            )
+            return dealt
+
+        def gather_words(name, table):
+            dealt = sb.tile([P, SLOTS], U32, name=name, align_bytes=64)
+            nc.vector.tensor_copy(
+                dealt[:].rearrange("p (r s) -> p s r", r=PACK), table[:].bitcast(U32).indirect(offsets[:])
+            )
+            return dealt
+
+        def interleave(copy, grouped, planes):
+            copy(
+                grouped.rearrange("p (c i t) -> p c t i", i=4, t=PACK),
+                planes.rearrange("p t (c i) -> p c t i", i=4),
+            )
+
+        def quantize(name, grouped, codes, scales):
+            nc.vector.quantize_mx(out=codes.bitcast(FP8X4), scales=scales, in_=grouped)
+
+        k_scale = gather_scales("k_scale", k_scale_table)
+        c_scale = gather_scales("c_scale", c_scale_table)
+
+        q_grouped = sb.tile([P, QUERIES * PACK], BF16, name="q_grouped", align_bytes=64)
+        interleave(nc.scalar.copy, q_grouped[:], q_raw[:])
+        k_codes = gather_words("k_codes", k_word_table)
+        q_codes = sb.tile([P, QUERIES], U32, name="q_codes", align_bytes=64)
+        q_scale = sb.tile([P, QUERIES], U8, name="q_scale", align_bytes=64)
+        quantize("q", q_grouped[:], q_codes[:], q_scale[:])
+        c_codes = gather_words("c_codes", c_word_table)
+
+        def first_layer(bank, codes, scale, row0, r):
+            acc = ps.tile([P, QUERIES], F32, name="acc%d" % bank, tag="bank%d" % bank)
+            cols = slice(r * P, (r + 1) * P)
+            nc.tensor.matmul_mx(
+                out=acc[:],
+                lhsT=codes[:, cols].bitcast(FP8X4),
+                lhsT_scale=scale[row0:, cols],
+                rhs=q_codes[:].bitcast(FP8X4),
+                rhs_scale=q_scale[:],
+                start=True,
+                stop=True,
+            )
+            return acc
+
+        gates = []
+        for r in range(PACK):
+            acc = first_layer(r, k_codes, k_scale, 0, r)
+            gate = sb.tile([P, QUERIES], F32, name="gate%d" % r)
+            nc.scalar.activation(gate[:], acc[:], SILU)
+            gates.append(gate)
+        y_planes = sb.tile([P, PACK, QUERIES], BF16, name="y_planes")
+        for r in range(PACK):
+            acc = first_layer(PACK + r, c_codes, c_scale, 4, r)
+            nc.vector.scalar_tensor_tensor(
+                y_planes[:, r, :], acc[:], slot_scale[:, r : r + 1], gates[r][:], MULT, MULT
+            )
+
+        def gather_values(j):
+            v_picked = sb.tile([P, SLOTS], BF16, name="v_picked%d" % j)
+            nc.vector.tensor_copy(v_picked[:], v_tables[j][:].indirect(offsets[:]))
+            pairs = v_picked[:].bitcast(F32)
+            turned = ps.tile([P, 2, P], F32, name="turned%d" % j, tag="bank%d" % j)
+            for u in range(2):
+                nc.tensor.transpose(turned[:, u, :], pairs[:, u::2], ident[:])
+            return turned
+
+        def group_values(j, turned):
+            v_grouped = sb.tile([P, P * PACK], BF16, name="v_grouped%d" % j, align_bytes=64)
+            nc.scalar.copy(
+                v_grouped[:].bitcast(F32).rearrange("p (e u) -> p e u", u=2), turned[:].rearrange("p u e -> p e u")
+            )
+            return v_grouped
+
+        half = QUERIES // 2
+        y_grouped = []
+        for h in range(2):
+            grouped = sb.tile([P, half * PACK], BF16, name="y_grouped%d" % h, align_bytes=64)
+            interleave(nc.scalar.copy, grouped[:], y_planes[:, :, h * half : (h + 1) * half])
+            y_grouped.append(grouped)
+        v_grouped = [group_values(j, gather_values(j)) for j in range(blocks - 1)]
+
+        codes = sb.tile([P, QUERIES + OUTPUTS], U32, name="codes", tag="v_table%d" % (blocks - 2), align_bytes=64)
+        y_codes = codes[:, :QUERIES]
+        y_scale = sb.tile([P, QUERIES], U8, name="y_scale", align_bytes=64)
+        for h in range(2):
+            cols = slice(h * half, (h + 1) * half)
+            quantize("y", y_grouped[h][:], y_codes[:, cols], y_scale[:, cols])
+
+        out_view = out[0].rearrange("(t p) e -> p t e", p=P)
+        for j in range(blocks):
+            last = j == blocks - 1
+            if last:
+                v_grouped.append(group_values(j, gather_values(j)))
+            v_codes = codes[:, QUERIES + j * P : QUERIES + (j + 1) * P]
+            v_scale = sb.tile([P, P], U8, name="v_scale%d" % j, align_bytes=64)
+            quantize("v", v_grouped[j][:], v_codes, v_scale[:])
+            parts = 2 if last else 1
+            per = q_tiles // parts
+            for part in range(parts):
+                acc = ps.tile([P, per, P], F32, name="res%d_%d" % (j, part), tag="bank%d" % ((4 + j + part) % 8))
+                for t in range(per):
+                    cols = slice((part * per + t) * P, (part * per + t + 1) * P)
+                    nc.tensor.matmul_mx(
+                        out=acc[:, t, :],
+                        lhsT=y_codes[:, cols].bitcast(FP8X4),
+                        lhsT_scale=y_scale[:, cols],
+                        rhs=v_codes.bitcast(FP8X4),
+                        rhs_scale=v_scale[:],
+                        start=True,
+                        stop=True,
+                    )
+                result = sb.tile([P, per, P], F32, name="result%d_%d" % (j, part))
+                if part == 0:
+                    nc.scalar.copy(result[:], acc[:])
+                else:
+                    nc.vector.tensor_copy(result[:], acc[:])
+                nc.sync.dma_start(out_view[:, part * per : (part + 1) * per, j * P : (j + 1) * P], result[:])

@@ -14,178 +14,203 @@ MULT = mybir.AluOpType.mult
 SILU = mybir.ActivationFunctionType.Silu
 
 P = 128
-PACK = 4
+PLACES = 4
+RUN = 8
 SLOTS = 512
+BLOCKS = SLOTS // (RUN * PLACES)
 NEURONS = 2048
+FEATURES = 512
 QUERIES = 512
 OUTPUTS = 512
-QUADRANTS = 4
-FLOPS = 3 * 2 * 512 * 512 * 512
+HALF = QUERIES // 2
+QUADRANT = 32
+K_SCALE_ROW = 0
+C_SCALE_ROW = 4
+ALIGN = 64
+FLOPS = 2 * 2 * FEATURES * SLOTS * QUERIES + 2 * SLOTS * QUERIES * OUTPUTS
 
 
 def tile_attend_mlp_swiglu_topk_kernel(tc, qT, k_words, k_scales, c_words, c_scales, vT, us, offs, out):
     nc = tc.nc
-    blocks = OUTPUTS // P
-    q_tiles = QUERIES // P
     with ExitStack() as ctx:
         sb = ctx.enter_context(tc.tile_pool(name="sb", bufs=1))
         ps = ctx.enter_context(tc.psum_pool(name="ps", bufs=1))
 
-        offsets = sb.tile([P, SLOTS // 16], U16, name="offsets")
-        nc.sync.dma_start(offsets[:], offs)
-        q_raw = sb.tile([P, PACK, QUERIES], F32, name="q_raw")
-        nc.sync.dma_start(q_raw[:], qT[0].rearrange("(p j) q -> p j q", j=PACK))
+        def load_queries(h):
+            q_raw = sb.tile([P, PLACES, HALF], F32, name="q_raw%d" % h)
+            nc.sync.dma_start(q_raw[:], qT[0].rearrange("(p r) q -> p r q", r=PLACES)[:, :, h * HALF : (h + 1) * HALF])
+            return q_raw
 
-        def load_scales(name, scales, row0):
+        def load_scales(name, scales, first_row):
             table = sb.tile([P, NEURONS], U8, name=name)
             nc.vector.memset(table[:].bitcast(I32), 0)
             rows = scales[0].bitcast(I32)
-            for quad in range(QUADRANTS):
-                first = 32 * quad + row0
-                queue = nc.gpsimd if quad == QUADRANTS - 1 else nc.scalar
-                queue.dma_start(table[first : first + 4, :].bitcast(I32), rows[4 * quad : 4 * quad + 4, :])
+            for quad in range(P // QUADRANT):
+                first = QUADRANT * quad + first_row
+                nc.sync.dma_start(table[first : first + 4, :].bitcast(I32), rows[4 * quad : 4 * quad + 4, :])
             return table
 
         def load_words(name, words):
-            table = sb.tile([P, NEURONS], I32, name=name)
-            nc.sync.dma_start(table[:], words[0].rearrange("p n t -> p (n t)").bitcast(I32))
+            table = sb.tile([P, NEURONS], I32, name=name, align_bytes=ALIGN)
+            nc.sync.dma_start(table[:], words[0].rearrange("p n r -> p (n r)").bitcast(I32))
             return table
 
-        k_scale_table = load_scales("k_scale_table", k_scales, 0)
+        q_raw = [load_queries(0)]
+        offsets = sb.tile([P, SLOTS // 16], U16, name="offsets")
+        nc.sync.dma_start(offsets[:], offs)
+        k_scale_table = load_scales("k_scale_table", k_scales, K_SCALE_ROW)
+        us_rows = sb.tile([P, P], F32, name="us_rows")
+        nc.gpsimd.memset(us_rows[:], 0.0)
+        nc.sync.dma_start(
+            us_rows[:PLACES, :].rearrange("r (g j) -> r g j", j=RUN),
+            us[0].rearrange("(g r j) o -> r g (j o)", r=PLACES, j=RUN),
+        )
         k_word_table = load_words("k_word_table", k_words)
-        c_scale_table = load_scales("c_scale_table", c_scales, 4)
+        c_scale_table = load_scales("c_scale_table", c_scales, C_SCALE_ROW)
         c_word_table = load_words("c_word_table", c_words)
-        slot_scale = sb.tile([P, PACK], F32, name="slot_scale")
-        nc.gpsimd.dma_start(slot_scale[:], us[0].rearrange("(p r) o -> p (r o)", r=PACK))
+        q_raw.append(load_queries(1))
         v_tables = []
-        for j in range(blocks):
-            v_table = sb.tile([P, NEURONS], F32, name="v_table%d" % j, tag="v_table%d" % j, align_bytes=64)
-            nc.sync.dma_start(v_table[:], vT[j * P : (j + 1) * P, :])
+        for n in range(OUTPUTS // P):
+            v_table = sb.tile([P, NEURONS], F32, name="v_table%d" % n, tag="v_table%d" % n, align_bytes=ALIGN)
+            nc.sync.dma_start(v_table[:], vT[n * P : (n + 1) * P, :])
             v_tables.append(v_table)
 
-        ident = sb.tile([P, P], F32, name="ident")
-        make_identity(nc, ident[:])
+        identity = sb.tile([P, P], F32, name="identity")
+        make_identity(nc, identity[:])
+        us_turned = ps.tile([P, P], F32, name="us_turned", tag="bank7")
+        nc.tensor.transpose(us_turned[:], us_rows[:], identity[:])
+        slot_scale = sb.tile([P, PLACES], F32, name="slot_scale")
+        nc.scalar.copy(slot_scale[:], us_turned[:, :PLACES])
+
+        def by_plane(columns):
+            return columns.rearrange("p (r g j) -> p g r j", r=PLACES, g=BLOCKS)
 
         def gather_scales(name, table):
-            picked = sb.tile([P, SLOTS], U8, name=name + "_picked")
+            picked = sb.tile([P, SLOTS], U8, name=name + "_picked", tag=name + "_picked", align_bytes=ALIGN)
             nc.vector.tensor_copy(picked[:], table[:].indirect(offsets[:]))
-            dealt = sb.tile([P, SLOTS], U8, name=name + "_dealt", align_bytes=64)
+            planes = sb.tile([P, SLOTS], U8, name=name, align_bytes=ALIGN)
             nc.vector.tensor_copy(
-                dealt[:].rearrange("p (r s) -> p s r", r=PACK), picked[:].rearrange("p (s r) -> p s r", r=PACK)
+                by_plane(planes[:].bitcast(I32)),
+                picked[:].bitcast(I32).rearrange("p (g r j) -> p g r j", r=PLACES, g=BLOCKS),
             )
-            return dealt
+            return planes
 
         def gather_words(name, table):
-            dealt = sb.tile([P, SLOTS], U32, name=name, align_bytes=64)
+            planes = sb.tile([P, SLOTS], U32, name=name, align_bytes=ALIGN)
+            nc.vector.tensor_copy(by_plane(planes[:]), table[:].bitcast(U32).indirect(offsets[:]))
+            return planes
+
+        def gather_values(n):
+            v_picked = sb.tile([P, SLOTS], BF16, name="v_picked%d" % n)
             nc.vector.tensor_copy(
-                dealt[:].rearrange("p (r s) -> p s r", r=PACK), table[:].bitcast(U32).indirect(offsets[:])
+                v_picked[:].rearrange("p (u g j s) -> p g u s j", u=2, j=RUN, s=2), v_tables[n][:].indirect(offsets[:])
             )
-            return dealt
+            return v_picked
 
-        def interleave(copy, grouped, planes):
-            copy(
-                grouped.rearrange("p (c i t) -> p c t i", i=4, t=PACK),
-                planes.rearrange("p t (c i) -> p c t i", i=4),
+        def weave(words, planes):
+            nc.scalar.copy(
+                words.rearrange("p (c i r) -> p c r i", i=4, r=PLACES), planes.rearrange("p r (c i) -> p c r i", i=4)
             )
 
-        def quantize(name, grouped, codes, scales):
-            nc.vector.quantize_mx(out=codes.bitcast(FP8X4), scales=scales, in_=grouped)
+        def quantize(words, codes, scale):
+            nc.vector.quantize_mx(out=codes.bitcast(FP8X4), scales=scale, in_=words)
 
-        k_scale = gather_scales("k_scale", k_scale_table)
-        c_scale = gather_scales("c_scale", c_scale_table)
-
-        q_grouped = sb.tile([P, QUERIES * PACK], BF16, name="q_grouped", align_bytes=64)
-        interleave(nc.scalar.copy, q_grouped[:], q_raw[:])
-        k_codes = gather_words("k_codes", k_word_table)
-        q_codes = sb.tile([P, QUERIES], U32, name="q_codes", align_bytes=64)
-        q_scale = sb.tile([P, QUERIES], U8, name="q_scale", align_bytes=64)
-        quantize("q", q_grouped[:], q_codes[:], q_scale[:])
-        c_codes = gather_words("c_codes", c_word_table)
-
-        def first_layer(bank, codes, scale, row0, r):
-            acc = ps.tile([P, QUERIES], F32, name="acc%d" % bank, tag="bank%d" % bank)
-            cols = slice(r * P, (r + 1) * P)
+        def product(acc, stationary, stationary_scale, moving, moving_scale):
             nc.tensor.matmul_mx(
-                out=acc[:],
-                lhsT=codes[:, cols].bitcast(FP8X4),
-                lhsT_scale=scale[row0:, cols],
-                rhs=q_codes[:].bitcast(FP8X4),
-                rhs_scale=q_scale[:],
+                out=acc,
+                lhsT=stationary.bitcast(FP8X4),
+                lhsT_scale=stationary_scale,
+                rhs=moving.bitcast(FP8X4),
+                rhs_scale=moving_scale,
                 start=True,
                 stop=True,
             )
-            return acc
 
-        gates = []
-        for r in range(PACK):
-            acc = first_layer(r, k_codes, k_scale, 0, r)
-            gate = sb.tile([P, QUERIES], F32, name="gate%d" % r)
-            nc.scalar.activation(gate[:], acc[:], SILU)
-            gates.append(gate)
-        y_planes = sb.tile([P, PACK, QUERIES], BF16, name="y_planes")
-        for r in range(PACK):
-            acc = first_layer(PACK + r, c_codes, c_scale, 4, r)
-            nc.vector.scalar_tensor_tensor(
-                y_planes[:, r, :], acc[:], slot_scale[:, r : r + 1], gates[r][:], MULT, MULT
-            )
+        k_scale = gather_scales("k_scale", k_scale_table)
+        k_codes = gather_words("k_codes", k_word_table)
+        q_codes, q_scale = [], []
+        for h, tag in enumerate(("k_scale_picked", "q_codes1")):
+            q_words = sb.tile([P, HALF * PLACES], BF16, name="q_words%d" % h, align_bytes=ALIGN)
+            weave(q_words[:], q_raw[h][:])
+            q_codes.append(sb.tile([P, HALF], U32, name="q_codes%d" % h, tag=tag, align_bytes=ALIGN))
+            q_scale.append(sb.tile([P, HALF], U8, name="q_scale%d" % h, align_bytes=ALIGN))
+            quantize(q_words[:], q_codes[h][:], q_scale[h][:])
+        c_scale = gather_scales("c_scale", c_scale_table)
+        c_codes = gather_words("c_codes", c_word_table)
 
-        def gather_values(j):
-            v_picked = sb.tile([P, SLOTS], BF16, name="v_picked%d" % j)
-            nc.vector.tensor_copy(v_picked[:], v_tables[j][:].indirect(offsets[:]))
-            pairs = v_picked[:].bitcast(F32)
-            turned = ps.tile([P, 2, P], F32, name="turned%d" % j, tag="bank%d" % j)
+        def first_layer(acc, codes, scale, first_row, h, r):
+            plane = slice(r * P, (r + 1) * P)
+            product(acc, codes[:, plane], scale[first_row:, plane], q_codes[h][:], q_scale[h][:])
+
+        gates = {}
+        for h in range(2):
             for u in range(2):
-                nc.tensor.transpose(turned[:, u, :], pairs[:, u::2], ident[:])
-            return turned
-
-        def group_values(j, turned):
-            v_grouped = sb.tile([P, P * PACK], BF16, name="v_grouped%d" % j, align_bytes=64)
-            nc.scalar.copy(
-                v_grouped[:].bitcast(F32).rearrange("p (e u) -> p e u", u=2), turned[:].rearrange("p u e -> p e u")
-            )
-            return v_grouped
-
-        half = QUERIES // 2
-        y_grouped = []
+                a_acc = ps.tile([P, 2, HALF], F32, name="a_acc%d_%d" % (h, u), tag="bank%d" % (2 * h + u))
+                for s in range(2):
+                    first_layer(a_acc[:, s, :], k_codes, k_scale, K_SCALE_ROW, h, 2 * u + s)
+                gates[h, u] = sb.tile([P, 2, HALF], F32, name="gate%d_%d" % (h, u))
+                nc.scalar.activation(gates[h, u][:], a_acc[:], SILU)
+        v_picked0 = gather_values(0)
+        y_words = sb.tile([P, 2, HALF * PLACES], BF16, name="y_words", tag="v_table0", align_bytes=ALIGN)
         for h in range(2):
-            grouped = sb.tile([P, half * PACK], BF16, name="y_grouped%d" % h, align_bytes=64)
-            interleave(nc.scalar.copy, grouped[:], y_planes[:, :, h * half : (h + 1) * half])
-            y_grouped.append(grouped)
-        v_grouped = [group_values(j, gather_values(j)) for j in range(blocks - 1)]
+            y_planes = sb.tile([P, PLACES, HALF], BF16, name="y_planes%d" % h)
+            for r in range(PLACES):
+                z_acc = ps.tile([P, HALF], F32, name="z_acc%d_%d" % (h, r), tag="bank%d" % (4 + r))
+                first_layer(z_acc[:], c_codes, c_scale, C_SCALE_ROW, h, r)
+                nc.vector.scalar_tensor_tensor(
+                    y_planes[:, r, :], z_acc[:], slot_scale[:, r : r + 1], gates[h, r // 2][:, r % 2, :], MULT, MULT
+                )
+            weave(y_words[:, h, :], y_planes[:])
 
-        codes = sb.tile([P, QUERIES + OUTPUTS], U32, name="codes", tag="v_table%d" % (blocks - 2), align_bytes=64)
-        y_codes = codes[:, :QUERIES]
-        y_scale = sb.tile([P, QUERIES], U8, name="y_scale", align_bytes=64)
-        for h in range(2):
-            cols = slice(h * half, (h + 1) * half)
-            quantize("y", y_grouped[h][:], y_codes[:, cols], y_scale[:, cols])
+        def turn_values(n, v_picked, v_words, copy):
+            pairs = v_picked[:].bitcast(F32)
+            turned = ps.tile([P, 2, P], F32, name="turned%d" % n, tag="bank%d" % n)
+            for u in range(2):
+                nc.tensor.transpose(turned[:, u, :], pairs[:, u * P : (u + 1) * P], identity[:])
+            copy(v_words.bitcast(F32).rearrange("p (e u) -> p e u", u=2), turned[:].rearrange("p u e -> p e u"))
+
+        v_words01 = sb.tile([P, 2 * P * PLACES], BF16, name="v_words01", align_bytes=ALIGN)
+        v_words2 = sb.tile([P, P * PLACES], BF16, name="v_words2", align_bytes=ALIGN)
+        v_words3 = sb.tile([P, P * PLACES], BF16, name="v_words3", align_bytes=ALIGN)
+        turn_values(0, v_picked0, v_words01[:, : P * PLACES], nc.scalar.copy)
+        turn_values(1, gather_values(1), v_words01[:, P * PLACES :], nc.scalar.copy)
+        turn_values(2, gather_values(2), v_words2[:], nc.scalar.copy)
+
+        early_codes = sb.tile([P, QUERIES + 2 * P], U32, name="early_codes", tag="v_table2", align_bytes=ALIGN)
+        y_codes = early_codes[:, :QUERIES]
+        y_scale = sb.tile([P, QUERIES], U8, name="y_scale", align_bytes=ALIGN)
+        quantize(y_words[:].rearrange("p h c -> p (h c)"), y_codes, y_scale[:])
 
         out_view = out[0].rearrange("(t p) e -> p t e", p=P)
-        for j in range(blocks):
-            last = j == blocks - 1
-            if last:
-                v_grouped.append(group_values(j, gather_values(j)))
-            v_codes = codes[:, QUERIES + j * P : QUERIES + (j + 1) * P]
-            v_scale = sb.tile([P, P], U8, name="v_scale%d" % j, align_bytes=64)
-            quantize("v", v_grouped[j][:], v_codes, v_scale[:])
-            parts = 2 if last else 1
-            per = q_tiles // parts
-            for part in range(parts):
-                acc = ps.tile([P, per, P], F32, name="res%d_%d" % (j, part), tag="bank%d" % ((4 + j + part) % 8))
-                for t in range(per):
-                    cols = slice((part * per + t) * P, (part * per + t + 1) * P)
-                    nc.tensor.matmul_mx(
-                        out=acc[:, t, :],
-                        lhsT=y_codes[:, cols].bitcast(FP8X4),
-                        lhsT_scale=y_scale[:, cols],
-                        rhs=v_codes.bitcast(FP8X4),
-                        rhs_scale=v_scale[:],
-                        start=True,
-                        stop=True,
-                    )
-                result = sb.tile([P, per, P], F32, name="result%d_%d" % (j, part))
-                if part == 0:
-                    nc.scalar.copy(result[:], acc[:])
-                else:
-                    nc.vector.tensor_copy(result[:], acc[:])
-                nc.sync.dma_start(out_view[:, part * per : (part + 1) * per, j * P : (j + 1) * P], result[:])
+
+        def quantize_values(name, v_words, v_codes):
+            v_scale = sb.tile([P, v_codes.shape[1]], U8, name=name, align_bytes=ALIGN)
+            quantize(v_words[:], v_codes, v_scale[:])
+            return v_codes, v_scale
+
+        def second_layer(bank, operand, first_output, query_tiles, copy):
+            v_codes, v_scale = operand
+            width = v_codes.shape[1]
+            out_acc = ps.tile([P, len(query_tiles), width], F32, name="out_acc%d" % bank, tag="bank%d" % bank)
+            for i, t in enumerate(query_tiles):
+                queries = slice(t * P, (t + 1) * P)
+                product(out_acc[:, i, :], y_codes[:, queries], y_scale[:, queries], v_codes, v_scale[:])
+            result = sb.tile([P, len(query_tiles), width], F32, name="result%d" % bank, align_bytes=ALIGN)
+            copy(result[:], out_acc[:])
+            nc.sync.dma_start(
+                out_view[:, query_tiles[0] : query_tiles[-1] + 1, first_output : first_output + width], result[:]
+            )
+
+        all_tiles = range(QUERIES // P)
+        low_tiles, high_tiles = all_tiles[:2], all_tiles[2:]
+        operand01 = quantize_values("v_scale01", v_words01, early_codes[:, QUERIES:])
+        second_layer(4, operand01, 0, low_tiles, nc.scalar.copy)
+        second_layer(5, operand01, 0, high_tiles, nc.scalar.copy)
+
+        turn_values(3, gather_values(3), v_words3[:], nc.vector.tensor_copy)
+        late_codes = sb.tile([P, 2, P], U32, name="late_codes", tag="v_table3", align_bytes=ALIGN)
+        operand2 = quantize_values("v_scale2", v_words2, late_codes[:, 0, :])
+        second_layer(6, operand2, 2 * P, all_tiles, nc.scalar.copy)
+        operand3 = quantize_values("v_scale3", v_words3, late_codes[:, 1, :])
+        second_layer(7, operand3, 3 * P, low_tiles, nc.scalar.copy)
+        second_layer(0, operand3, 3 * P, high_tiles, nc.vector.tensor_copy)

from contextlib import ExitStack

import concourse.mybir as mybir
from concourse.masks import make_identity

F32 = mybir.dt.float32
BF16 = mybir.dt.bfloat16
I32 = mybir.dt.int32
U32 = mybir.dt.uint32
U16 = mybir.dt.uint16
U8 = mybir.dt.uint8
FP8X4 = mybir.dt.float8_e4m3fn_x4
MULT = mybir.AluOpType.mult
SILU = mybir.ActivationFunctionType.Silu

P = 128
PLACES = 4
RUN = 8
SLOTS = 512
BLOCKS = SLOTS // (RUN * PLACES)
NEURONS = 2048
FEATURES = 512
QUERIES = 512
OUTPUTS = 512
HALF = QUERIES // 2
QUADRANT = 32
K_SCALE_ROW = 0
C_SCALE_ROW = 4
ALIGN = 64
FLOPS = 2 * 2 * FEATURES * SLOTS * QUERIES + 2 * SLOTS * QUERIES * OUTPUTS


def tile_attend_mlp_swiglu_topk_kernel(tc, qT, k_words, k_scales, c_words, c_scales, vT, us, offs, out):
    nc = tc.nc
    with ExitStack() as ctx:
        sb = ctx.enter_context(tc.tile_pool(name="sb", bufs=1))
        ps = ctx.enter_context(tc.psum_pool(name="ps", bufs=1))

        def load_queries(h):
            q_raw = sb.tile([P, PLACES, HALF], F32, name="q_raw%d" % h)
            nc.sync.dma_start(q_raw[:], qT[0].rearrange("(p r) q -> p r q", r=PLACES)[:, :, h * HALF : (h + 1) * HALF])
            return q_raw

        def load_scales(name, scales, first_row):
            table = sb.tile([P, NEURONS], U8, name=name)
            nc.vector.memset(table[:].bitcast(I32), 0)
            rows = scales[0].bitcast(I32)
            for quad in range(P // QUADRANT):
                first = QUADRANT * quad + first_row
                nc.sync.dma_start(table[first : first + 4, :].bitcast(I32), rows[4 * quad : 4 * quad + 4, :])
            return table

        def load_words(name, words):
            table = sb.tile([P, NEURONS], I32, name=name, align_bytes=ALIGN)
            nc.sync.dma_start(table[:], words[0].rearrange("p n r -> p (n r)").bitcast(I32))
            return table

        q_raw = [load_queries(0)]
        offsets = sb.tile([P, SLOTS // 16], U16, name="offsets")
        nc.sync.dma_start(offsets[:], offs)
        k_scale_table = load_scales("k_scale_table", k_scales, K_SCALE_ROW)
        us_rows = sb.tile([P, P], F32, name="us_rows")
        nc.gpsimd.memset(us_rows[:], 0.0)
        nc.sync.dma_start(
            us_rows[:PLACES, :].rearrange("r (g j) -> r g j", j=RUN),
            us[0].rearrange("(g r j) o -> r g (j o)", r=PLACES, j=RUN),
        )
        k_word_table = load_words("k_word_table", k_words)
        c_scale_table = load_scales("c_scale_table", c_scales, C_SCALE_ROW)
        c_word_table = load_words("c_word_table", c_words)
        q_raw.append(load_queries(1))
        v_tables = []
        for n in range(OUTPUTS // P):
            v_table = sb.tile([P, NEURONS], F32, name="v_table%d" % n, tag="v_table%d" % n, align_bytes=ALIGN)
            nc.sync.dma_start(v_table[:], vT[n * P : (n + 1) * P, :])
            v_tables.append(v_table)

        identity = sb.tile([P, P], F32, name="identity")
        make_identity(nc, identity[:])
        us_turned = ps.tile([P, P], F32, name="us_turned", tag="bank7")
        nc.tensor.transpose(us_turned[:], us_rows[:], identity[:])
        slot_scale = sb.tile([P, PLACES], F32, name="slot_scale")
        nc.scalar.copy(slot_scale[:], us_turned[:, :PLACES])

        def by_plane(columns):
            return columns.rearrange("p (r g j) -> p g r j", r=PLACES, g=BLOCKS)

        def gather_scales(name, table):
            picked = sb.tile([P, SLOTS], U8, name=name + "_picked", tag=name + "_picked", align_bytes=ALIGN)
            nc.vector.tensor_copy(picked[:], table[:].indirect(offsets[:]))
            planes = sb.tile([P, SLOTS], U8, name=name, align_bytes=ALIGN)
            nc.vector.tensor_copy(
                by_plane(planes[:].bitcast(I32)),
                picked[:].bitcast(I32).rearrange("p (g r j) -> p g r j", r=PLACES, g=BLOCKS),
            )
            return planes

        def gather_words(name, table):
            planes = sb.tile([P, SLOTS], U32, name=name, align_bytes=ALIGN)
            nc.vector.tensor_copy(by_plane(planes[:]), table[:].bitcast(U32).indirect(offsets[:]))
            return planes

        def gather_values(n):
            v_picked = sb.tile([P, SLOTS], BF16, name="v_picked%d" % n)
            nc.vector.tensor_copy(
                v_picked[:].rearrange("p (u g j s) -> p g u s j", u=2, j=RUN, s=2), v_tables[n][:].indirect(offsets[:])
            )
            return v_picked

        def weave(words, planes):
            nc.scalar.copy(
                words.rearrange("p (c i r) -> p c r i", i=4, r=PLACES), planes.rearrange("p r (c i) -> p c r i", i=4)
            )

        def quantize(words, codes, scale):
            nc.vector.quantize_mx(out=codes.bitcast(FP8X4), scales=scale, in_=words)

        def product(acc, stationary, stationary_scale, moving, moving_scale):
            nc.tensor.matmul_mx(
                out=acc,
                lhsT=stationary.bitcast(FP8X4),
                lhsT_scale=stationary_scale,
                rhs=moving.bitcast(FP8X4),
                rhs_scale=moving_scale,
                start=True,
                stop=True,
            )

        k_scale = gather_scales("k_scale", k_scale_table)
        k_codes = gather_words("k_codes", k_word_table)
        q_codes, q_scale = [], []
        for h, tag in enumerate(("k_scale_picked", "q_codes1")):
            q_words = sb.tile([P, HALF * PLACES], BF16, name="q_words%d" % h, align_bytes=ALIGN)
            weave(q_words[:], q_raw[h][:])
            q_codes.append(sb.tile([P, HALF], U32, name="q_codes%d" % h, tag=tag, align_bytes=ALIGN))
            q_scale.append(sb.tile([P, HALF], U8, name="q_scale%d" % h, align_bytes=ALIGN))
            quantize(q_words[:], q_codes[h][:], q_scale[h][:])
        c_scale = gather_scales("c_scale", c_scale_table)
        c_codes = gather_words("c_codes", c_word_table)

        def first_layer(acc, codes, scale, first_row, h, r):
            plane = slice(r * P, (r + 1) * P)
            product(acc, codes[:, plane], scale[first_row:, plane], q_codes[h][:], q_scale[h][:])

        gates = {}
        for h in range(2):
            for u in range(2):
                a_acc = ps.tile([P, 2, HALF], F32, name="a_acc%d_%d" % (h, u), tag="bank%d" % (2 * h + u))
                for s in range(2):
                    first_layer(a_acc[:, s, :], k_codes, k_scale, K_SCALE_ROW, h, 2 * u + s)
                gates[h, u] = sb.tile([P, 2, HALF], F32, name="gate%d_%d" % (h, u))
                nc.scalar.activation(gates[h, u][:], a_acc[:], SILU)
        v_picked0 = gather_values(0)
        y_words = sb.tile([P, 2, HALF * PLACES], BF16, name="y_words", tag="v_table0", align_bytes=ALIGN)
        for h in range(2):
            y_planes = sb.tile([P, PLACES, HALF], BF16, name="y_planes%d" % h)
            for r in range(PLACES):
                z_acc = ps.tile([P, HALF], F32, name="z_acc%d_%d" % (h, r), tag="bank%d" % (4 + r))
                first_layer(z_acc[:], c_codes, c_scale, C_SCALE_ROW, h, r)
                nc.vector.scalar_tensor_tensor(
                    y_planes[:, r, :], z_acc[:], slot_scale[:, r : r + 1], gates[h, r // 2][:, r % 2, :], MULT, MULT
                )
            weave(y_words[:, h, :], y_planes[:])

        def turn_values(n, v_picked, v_words, copy):
            pairs = v_picked[:].bitcast(F32)
            turned = ps.tile([P, 2, P], F32, name="turned%d" % n, tag="bank%d" % n)
            for u in range(2):
                nc.tensor.transpose(turned[:, u, :], pairs[:, u * P : (u + 1) * P], identity[:])
            copy(v_words.bitcast(F32).rearrange("p (e u) -> p e u", u=2), turned[:].rearrange("p u e -> p e u"))

        v_words01 = sb.tile([P, 2 * P * PLACES], BF16, name="v_words01", align_bytes=ALIGN)
        v_words2 = sb.tile([P, P * PLACES], BF16, name="v_words2", align_bytes=ALIGN)
        v_words3 = sb.tile([P, P * PLACES], BF16, name="v_words3", align_bytes=ALIGN)
        turn_values(0, v_picked0, v_words01[:, : P * PLACES], nc.scalar.copy)
        turn_values(1, gather_values(1), v_words01[:, P * PLACES :], nc.scalar.copy)
        turn_values(2, gather_values(2), v_words2[:], nc.scalar.copy)

        early_codes = sb.tile([P, QUERIES + 2 * P], U32, name="early_codes", tag="v_table2", align_bytes=ALIGN)
        y_codes = early_codes[:, :QUERIES]
        y_scale = sb.tile([P, QUERIES], U8, name="y_scale", align_bytes=ALIGN)
        quantize(y_words[:].rearrange("p h c -> p (h c)"), y_codes, y_scale[:])

        out_view = out[0].rearrange("(t p) e -> p t e", p=P)

        def quantize_values(name, v_words, v_codes):
            v_scale = sb.tile([P, v_codes.shape[1]], U8, name=name, align_bytes=ALIGN)
            quantize(v_words[:], v_codes, v_scale[:])
            return v_codes, v_scale

        def second_layer(bank, operand, first_output, query_tiles, copy):
            v_codes, v_scale = operand
            width = v_codes.shape[1]
            out_acc = ps.tile([P, len(query_tiles), width], F32, name="out_acc%d" % bank, tag="bank%d" % bank)
            for i, t in enumerate(query_tiles):
                queries = slice(t * P, (t + 1) * P)
                product(out_acc[:, i, :], y_codes[:, queries], y_scale[:, queries], v_codes, v_scale[:])
            result = sb.tile([P, len(query_tiles), width], F32, name="result%d" % bank, align_bytes=ALIGN)
            copy(result[:], out_acc[:])
            nc.sync.dma_start(
                out_view[:, query_tiles[0] : query_tiles[-1] + 1, first_output : first_output + width], result[:]
            )

        all_tiles = range(QUERIES // P)
        low_tiles, high_tiles = all_tiles[:2], all_tiles[2:]
        operand01 = quantize_values("v_scale01", v_words01, early_codes[:, QUERIES:])
        second_layer(4, operand01, 0, low_tiles, nc.scalar.copy)
        second_layer(5, operand01, 0, high_tiles, nc.scalar.copy)

        turn_values(3, gather_values(3), v_words3[:], nc.vector.tensor_copy)
        late_codes = sb.tile([P, 2, P], U32, name="late_codes", tag="v_table3", align_bytes=ALIGN)
        operand2 = quantize_values("v_scale2", v_words2, late_codes[:, 0, :])
        second_layer(6, operand2, 2 * P, all_tiles, nc.scalar.copy)
        operand3 = quantize_values("v_scale3", v_words3, late_codes[:, 1, :])
        second_layer(7, operand3, 3 * P, low_tiles, nc.scalar.copy)
        second_layer(0, operand3, 3 * P, high_tiles, nc.vector.tensor_copy)
